import numpy as np
import ml_dtypes


def mxq(x, axis, fmt="e4m3"):
    dtype, down = {"e4m3": (ml_dtypes.float8_e4m3fn, 7), "e5m2": (ml_dtypes.float8_e5m2, 14)}[fmt]
    v = np.moveaxis(np.asarray(x, np.float32).astype(ml_dtypes.bfloat16).astype(np.float64), axis, -1)
    blocks = v.reshape(v.shape[:-1] + (-1, 32))
    amax = np.abs(blocks).max(-1, keepdims=True)
    byte = np.maximum(np.where(amax > 0, np.frexp(amax)[1] - 1 + 127, 0) - down, 1)
    scale = np.exp2(byte - 127.0)
    codes = (blocks / scale).astype(np.float32).astype(dtype).astype(np.float64)
    return np.moveaxis((codes * scale).reshape(v.shape), -1, axis)


WIDE = False


def mx_kscale(k):
    if not WIDE:
        return np.ones(k)
    levels = np.array([10, -10, 5, -5, 0])
    if k % 512:
        return np.exp2(np.random.permutation(np.resize(levels, k // 32))).repeat(32)
    a = np.empty((k // 512, 16))
    for p in range(k // 512):
        a[p, :8] = np.random.permutation(np.resize(levels, 8))
        for g in range(8):
            far = levels[np.abs(levels - a[p, g]) >= 10]
            a[p, g + 8] = far[np.random.randint(len(far))]
    return np.exp2(a.ravel()).repeat(32)


def f64(x):
    return np.asarray(x).astype(np.float64)


def striped(idx):
    return np.tile(idx.reshape(-1, 16).T, (8, 1)).astype(np.uint16)


def unstriped(offs):
    return offs[:16].T.reshape(-1).astype(np.int64)


E2M1 = np.array([0.0, 0.5, 1.0, 1.5, 2.0, 3.0, 4.0, 6.0, -0.0, -0.5, -1.0, -1.5, -2.0, -3.0, -4.0, -6.0])


def pack_weight(w, fmt):
    k, n = w.shape
    w = f64(np.asarray(w, np.float32).astype(ml_dtypes.bfloat16)).reshape(k // 32, 32, n)
    amax = np.abs(w).max(1)
    if fmt == "e4m3":
        byte = np.frexp(amax)[1] - 1 + 127 - 7
    else:
        mant, ex = np.frexp(amax / 6.0)
        byte = np.where(mant > 0.5, ex, ex - 1) + 127
    byte = np.clip(np.where(amax > 0, byte, 1), 1, 254)
    scaled = (w * np.exp2(127.0 - byte)[:, None, :]).reshape(k, n).astype(np.float32)
    by_word = np.ascontiguousarray(scaled.reshape(k // 512, 128, 4, n).transpose(0, 1, 3, 2))
    if fmt == "e4m3":
        words = by_word.astype(ml_dtypes.float8_e4m3fn).view(np.uint8)
    else:
        c = by_word.astype(ml_dtypes.float4_e2m1fn).view(np.uint8) & 0xF
        words = (c[..., 0::2] | (c[..., 1::2] << 4)).reshape(k // 512, 128, 2 * n)
    return np.ascontiguousarray(words), np.ascontiguousarray(byte.astype(np.uint8).reshape(k // 512, 16, n))


def unpack_weight(words, scales, fmt):
    g, _, n = scales.shape
    words = np.ascontiguousarray(words).reshape(g, 128, n, -1)
    if fmt == "e4m3":
        vals = words.view(ml_dtypes.float8_e4m3fn).astype(np.float64)
    else:
        nib = np.empty((g, 128, n, 4), np.uint8)
        nib[..., 0::2] = words & 0xF
        nib[..., 1::2] = words >> 4
        vals = E2M1[nib]
    vals = vals * np.repeat(np.exp2(scales.astype(np.float64) - 127.0), 8, axis=1)[..., None]
    return vals.transpose(0, 1, 3, 2).reshape(g * 512, n)


def gelu(v):
    return 0.5 * v * (1.0 + np.tanh(np.sqrt(2.0 / np.pi) * (v + 0.044715 * v**3)))


K, H, N, T, S, P, P2 = 1024, 512, 384, 4096, 2048, 1024, 512


def setup_inputs():
    n = np.random.standard_normal
    s = mx_kscale(K)[:, None]
    u = mx_kscale(H)[:, None]
    tab_words, tab_scales = pack_weight(n((K, T)) * s, "e4m3")
    w1 = (n((K, H)) / np.sqrt(K) / s * u.T).astype(np.float32)
    w2_words, w2_scales = pack_weight(n((K, H)) / np.sqrt(K) / s * u.T, "e2m1")
    w3 = (n((H, N)) / np.sqrt(H) / u).astype(np.float32)
    w4_words, w4_scales = pack_weight(n((H, N)) / np.sqrt(H) / u, "e2m1")
    sharp = (1.2 * np.exp(0.3 * n(H)) / u[:, 0]).astype(np.float32)
    wf = (np.sign(n(N)) * np.exp(0.3 * n(N))).astype(np.float32)
    offs = striped(np.random.permutation(T)[:S])
    pos1 = striped(np.random.permutation(S)[:P])
    pos2 = striped(np.random.permutation(S)[:P])
    pos3 = striped(np.random.permutation(P)[:P2])
    pos4 = striped(np.random.permutation(S)[:P2])
    return dict(tab_words=tab_words, tab_scales=tab_scales, offs=offs, w1=w1,
                w2_words=w2_words, w2_scales=w2_scales, sharp=sharp,
                pos1=pos1, pos2=pos2, pos3=pos3, pos4=pos4, w3=w3,
                w4_words=w4_words, w4_scales=w4_scales, wf=wf)


def reference(tab_words, tab_scales, offs, w1, w2_words, w2_scales, sharp,
              pos1, pos2, pos3, pos4, w3, w4_words, w4_scales, wf):
    v = unpack_weight(tab_words, tab_scales, "e4m3")[:, unstriped(offs)]
    w1q = mxq(f64(w1), 0, "e4m3")
    w2 = unpack_weight(w2_words, w2_scales, "e2m1")
    h = np.maximum(w1q.T @ v, w2.T @ v)
    bend = np.tanh(f64(sharp)[:, None] * h[:, unstriped(pos2)])
    a1 = h[:, unstriped(pos1)] * bend
    a2 = a1[:, unstriped(pos3)] + h[:, unstriped(pos4)]
    a2q = mxq(a2, 0, "e4m3")
    w3q = mxq(f64(w3), 0, "e4m3")
    w4 = unpack_weight(w4_words, w4_scales, "e2m1")
    top = np.maximum(w3q.T @ a2q, w4.T @ a2q)
    return f64(wf)[:, None] * top

@@ -1,0 +1,265 @@
+from contextlib import ExitStack
+
+import concourse.mybir as mybir
+
+K, H, N, T, S, PAIRS, KEPT = 1024, 512, 384, 4096, 2048, 1024, 512
+FLOPS = 2 * 2 * K * H * S + 2 * 2 * H * N * KEPT
+
+F32 = mybir.dt.float32
+BF16 = mybir.dt.bfloat16
+I32 = mybir.dt.int32
+U32 = mybir.dt.uint32
+U16 = mybir.dt.uint16
+U8 = mybir.dt.uint8
+FP8X4 = mybir.dt.float8_e4m3fn_x4
+FP4X4 = mybir.dt.float4_e2m1fn_x4
+ALU = mybir.AluOpType
+ACT = mybir.ActivationFunctionType
+
+P = 128
+PACK = 4
+PASSES = K // (P * PACK)
+BANK = 512
+SLICES = S // BANK
+PER_COL = 16
+OUT_BLOCKS = N // P
+PIECE = 128
+PIECES = KEPT // PIECE
+LIVE0 = 96
+
+
+def tile_list_duplicate_claim_flags_kernel(
+    tc, tab_words, tab_scales, offs, w1, w2_words, w2_scales, sharp,
+    pos1, pos2, pos3, pos4, w3, w4_words, w4_scales, wf, out,
+):
+    nc = tc.nc
+    with ExitStack() as ctx:
+        keep = ctx.enter_context(tc.tile_pool(name="keep", bufs=1))
+        ring = ctx.enter_context(tc.tile_pool(name="ring", bufs=2))
+        psum = ctx.enter_context(tc.psum_pool(name="psum", bufs=8))
+
+        def scale_rows(dst, src, queue):
+            nc.vector.memset(dst[:].rearrange("p a n -> p (a n)").bitcast(I32), 0)
+            for q in range(4):
+                queue.dma_start(
+                    out=dst[32 * q : 32 * q + 4, :, :].bitcast(I32),
+                    in_=src[:, 4 * q : 4 * q + 4, :].rearrange("a r n -> r a n").bitcast(I32),
+                )
+
+        w2_scale_raw = keep.tile([P, PASSES, H], U8, align_bytes=64)
+        scale_rows(w2_scale_raw, w2_scales, nc.scalar)
+        scale_window = keep.tile([P, T], U8, tag="scale_window_then_w1", align_bytes=64)
+        nc.vector.memset(scale_window[0:LIVE0, :].bitcast(I32), 0)
+        nc.sync.dma_start(
+            out=scale_window[LIVE0:P, :].bitcast(I32),
+            in_=tab_scales.rearrange("a q t -> (a q) t").bitcast(I32),
+        )
+        idx = keep.tile([P, S // PER_COL], U16)
+        nc.sync.dma_start(idx[:], offs)
+
+        def load_words(a):
+            words = keep.tile([P, T], I32, name="words%d" % a, tag="words%d" % a, align_bytes=64)
+            nc.sync.dma_start(out=words[:], in_=tab_words[a].rearrange("p t i -> p (t i)").bitcast(I32))
+            return words
+
+        def load_w1(a, tag):
+            raw = keep.tile([P, PACK, H], F32, name="w1_raw%d" % a, tag=tag, align_bytes=64)
+            nc.sync.dma_start(
+                out=raw[:], in_=w1[a * P * PACK : (a + 1) * P * PACK, :].rearrange("(p j) c -> p j c", j=PACK)
+            )
+            return raw
+
+        p2 = keep.tile([P, PAIRS // PER_COL], U16)
+        nc.sync.dma_start(p2[:], pos2)
+        p4 = keep.tile([P, KEPT // PER_COL], U16)
+        nc.sync.dma_start(p4[:], pos4)
+        p1 = keep.tile([P, PAIRS // PER_COL], U16)
+        nc.sync.dma_start(p1[:], pos1)
+        p3 = keep.tile([P, KEPT // PER_COL], U16)
+        nc.sync.dma_start(p3[:], pos3)
+        word_windows = [load_words(0)]
+        w2_raw = keep.tile([P, PASSES, 2 * H], U8, align_bytes=64)
+        nc.sync.dma_start(out=w2_raw[:].bitcast(I32), in_=w2_words.rearrange("a p n -> p a n").bitcast(I32))
+        w1_raw = [load_w1(0, "w1_then_w4")]
+        word_windows.append(load_words(1))
+
+        v_scales = keep.tile([P, PASSES, S], U8, align_bytes=64)
+        nc.gpsimd.memset(v_scales[:].rearrange("p a n -> p (a n)").bitcast(I32), 0)
+        sharp_sb = keep.tile([P, PACK], F32)
+        nc.gpsimd.dma_start(out=sharp_sb[:], in_=sharp.rearrange("(p t) -> p t", t=PACK))
+        w4_scale = keep.tile([P, 1, N], U8, align_bytes=64)
+        scale_rows(w4_scale, w4_scales, nc.gpsimd)
+        wf_sb = keep.tile([P, OUT_BLOCKS], F32)
+        with nc.allow_non_contiguous_dma(reason="one weight for each output row"):
+            nc.gpsimd.dma_start(out=wf_sb[:], in_=wf.rearrange("(b p) -> p b", p=P))
+
+        picked_scales = keep.tile([P, S], U8, align_bytes=64)
+        nc.vector.tensor_copy(picked_scales[:], scale_window[:].indirect(idx[:]))
+
+        def place_scales(a):
+            for q in range(4):
+                row = LIVE0 + 16 * a + 4 * q
+                nc.sync.dma_start(
+                    out=v_scales[32 * q : 32 * q + 4, a, :].bitcast(I32),
+                    in_=picked_scales[row : row + 4, :].bitcast(I32),
+                )
+
+        place_scales(0)
+        w1_raw.append(load_w1(1, "scale_window_then_w1"))
+        place_scales(1)
+
+        v_words = {}
+
+        def gather_words(a, s):
+            picked = keep.tile([P, BANK], U32, name="v_words%d_%d" % (a, s), align_bytes=64)
+            cols = BANK // PER_COL
+            nc.vector.tensor_copy(
+                picked[:], word_windows[a][:].bitcast(U32).indirect(idx[:, s * cols : (s + 1) * cols])
+            )
+            v_words[a, s] = picked
+
+        w1_codes, w1_scale = {}, {}
+
+        def quantise_w1(a, t):
+            grouped = ring.tile([P, P, PACK], BF16, name="w1_grouped", bufs=4, align_bytes=64)
+            nc.scalar.copy(out=grouped[:], in_=w1_raw[a][:].rearrange("p j (m t) -> p t m j", t=PACK)[:, t, :, :])
+            codes = keep.tile([P, P], U32, name="w1_codes%d_%d" % (a, t), align_bytes=64)
+            scale = keep.tile([P, P], U8, name="w1_scale%d_%d" % (a, t), align_bytes=64)
+            nc.vector.quantize_mx(
+                out=codes[:].bitcast(FP8X4), scales=scale[:], in_=grouped[:].rearrange("p m j -> p (m j)")
+            )
+            w1_codes[a, t], w1_scale[a, t] = codes, scale
+
+        for s in range(SLICES):
+            gather_words(0, s)
+
+        w2_codes = keep.tile([P, PASSES, PACK, 2 * P], U8, align_bytes=64)
+        w2_scale = keep.tile([P, PASSES, PACK, P], U8, align_bytes=64)
+        nc.vector.tensor_copy(
+            out=w2_codes[:].bitcast(U16), in_=w2_raw[:].bitcast(U16).rearrange("p a (m t) -> p a t m", t=PACK)
+        )
+        nc.vector.tensor_copy(out=w2_scale[:], in_=w2_scale_raw[:].rearrange("p a (m t) -> p a t m", t=PACK))
+        for t in range(PACK):
+            quantise_w1(0, t)
+        for s in range(SLICES):
+            gather_words(1, s)
+        for t in range(PACK):
+            quantise_w1(1, t)
+
+        w3_raw = keep.tile([P, PACK, N], F32, tag="words0", align_bytes=64)
+        nc.sync.dma_start(out=w3_raw[:], in_=w3.rearrange("(p j) n -> p j n", j=PACK))
+        w4_codes = keep.tile([P, 2 * N], U8, tag="w1_then_w4", align_bytes=64)
+        nc.sync.dma_start(out=w4_codes[:].bitcast(I32), in_=w4_words[0].bitcast(I32))
+
+        h = [keep.tile([P, S], F32, name="h%d" % t) for t in range(PACK)]
+
+        def first_pass(t, s, a, by_w1, by_w2):
+            cols = slice(s * BANK, (s + 1) * BANK)
+            nc.tensor.matmul_mx(
+                out=by_w2[:], lhsT=w2_codes[:, a, t, :].bitcast(FP4X4), lhsT_scale=w2_scale[:, a, t, :],
+                rhs=v_words[a, s][:].bitcast(FP8X4), rhs_scale=v_scales[:, a, cols],
+                start=(a == 0), stop=(a == PASSES - 1),
+            )
+            nc.tensor.matmul_mx(
+                out=by_w1[:], lhsT=w1_codes[a, t][:].bitcast(FP8X4), lhsT_scale=w1_scale[a, t][:],
+                rhs=v_words[a, s][:].bitcast(FP8X4), rhs_scale=v_scales[:, a, cols],
+                start=(a == 0), stop=(a == PASSES - 1),
+            )
+
+        def h_slice(t, s):
+            by_w1 = psum.tile([P, BANK], F32, name="bank")
+            by_w2 = psum.tile([P, BANK], F32, name="bank")
+            for a in range(PASSES):
+                first_pass(t, s, a, by_w1, by_w2)
+            by_w2_sb = ring.tile([P, BANK], F32, name="by_w2_sb", bufs=4)
+            nc.scalar.copy(out=by_w2_sb[:], in_=by_w2[:])
+            nc.vector.tensor_tensor(h[t][:, s * BANK : (s + 1) * BANK], by_w1[:], by_w2_sb[:], ALU.max)
+
+        for s in range(SLICES):
+            h_slice(0, s)
+
+        a2 = [keep.tile([P, 2, KEPT], F32, name="a2_%d" % u) for u in range(2)]
+        a2_grouped = [keep.tile([P, PIECE, PACK], BF16, name="a2_grouped%d" % q, align_bytes=64) for q in range(PIECES)]
+
+        def round_pair(u, q):
+            nc.scalar.copy(
+                out=a2_grouped[q][:, :, 2 * u : 2 * u + 2],
+                in_=a2[u][:, :, q * PIECE : (q + 1) * PIECE].rearrange("p e j -> p j e"),
+            )
+
+        w3_codes = keep.tile([P, N], U32, align_bytes=64)
+        w3_scale = keep.tile([P, N], U8, align_bytes=64)
+
+        def quantise_w3():
+            grouped = keep.tile([P, N, PACK], BF16, name="w3_grouped", align_bytes=64)
+            nc.scalar.copy(
+                out=grouped[:].rearrange("p (c i) j -> p c j i", i=4),
+                in_=w3_raw[:].rearrange("p j (c i) -> p c j i", i=4),
+            )
+            nc.vector.quantize_mx(
+                out=w3_codes[:].bitcast(FP8X4), scales=w3_scale[:], in_=grouped[:].rearrange("p n j -> p (n j)")
+            )
+
+        def flags(q):
+            codes = ring.tile([P, PIECE], U32, name="a2_codes", align_bytes=64)
+            scale = ring.tile([P, PIECE], U8, name="a2_scale", align_bytes=64)
+            nc.vector.quantize_mx(
+                out=codes[:].bitcast(FP8X4), scales=scale[:], in_=a2_grouped[q][:].rearrange("p j t -> p (j t)")
+            )
+            by_w3 = psum.tile([P, OUT_BLOCKS, PIECE], F32, name="bank")
+            by_w4 = psum.tile([P, OUT_BLOCKS, PIECE], F32, name="bank")
+            for b in range(OUT_BLOCKS):
+                nc.tensor.matmul_mx(
+                    out=by_w4[:, b, :], lhsT=w4_codes[:, 2 * P * b : 2 * P * (b + 1)].bitcast(FP4X4),
+                    lhsT_scale=w4_scale[:, 0, P * b : P * (b + 1)],
+                    rhs=codes[:].bitcast(FP8X4), rhs_scale=scale[:], start=True, stop=True,
+                )
+            for b in range(OUT_BLOCKS):
+                nc.tensor.matmul_mx(
+                    out=by_w3[:, b, :], lhsT=w3_codes[:, P * b : P * (b + 1)].bitcast(FP8X4),
+                    lhsT_scale=w3_scale[:, P * b : P * (b + 1)],
+                    rhs=codes[:].bitcast(FP8X4), rhs_scale=scale[:], start=True, stop=True,
+                )
+            by_w4_sb = ring.tile([P, OUT_BLOCKS, PIECE], F32, name="by_w4_sb")
+            nc.scalar.copy(out=by_w4_sb[:], in_=by_w4[:])
+            top = ring.tile([P, OUT_BLOCKS, PIECE], F32, name="top")
+            nc.vector.tensor_tensor(top[:], by_w3[:], by_w4_sb[:], ALU.max)
+            weighted = ring.tile([P, OUT_BLOCKS, PIECE], F32, name="weighted", bufs=4)
+            for b in range(OUT_BLOCKS):
+                nc.scalar.activation(out=weighted[:, b, :], in_=top[:, b, :], func=ACT.Copy, scale=wf_sb[:, b : b + 1])
+            nc.sync.dma_start(
+                out=out.rearrange("(b p) j -> p b j", p=P)[:, :, q * PIECE : (q + 1) * PIECE], in_=weighted[:]
+            )
+
+        for t in range(PACK):
+            last = t == PACK - 1
+            second = ring.tile([P, PAIRS], F32, name="second")
+            nc.vector.tensor_copy(second[:], h[t][:].indirect(p2[:]))
+            bend = ring.tile([P, PAIRS], F32, name="bend")
+            nc.scalar.activation(out=bend[:], in_=second[:], func=ACT.Tanh, scale=sharp_sb[:, t : t + 1])
+            receipt = ring.tile([P, KEPT], F32, name="receipt")
+            nc.vector.tensor_copy(receipt[:], h[t][:].indirect(p4[:]))
+            if not last:
+                for s in range(SLICES // 2):
+                    h_slice(t + 1, s)
+            a1 = ring.tile([P, PAIRS], F32, name="a1")
+            nc.vector.tensor_tensor(a1[:], h[t][:].indirect(p1[:]), bend[:], ALU.mult)
+            if not last:
+                for s in range(SLICES // 2, SLICES):
+                    h_slice(t + 1, s)
+                nc.vector.tensor_tensor(a2[t // 2][:, t % 2, :], a1[:].indirect(p3[:]), receipt[:], ALU.add)
+            if t == 1:
+                for q in range(PIECES):
+                    round_pair(0, q)
+                quantise_w3()
+            if last:
+                cols = PIECE // PER_COL
+                for q in range(PIECES):
+                    part = slice(q * PIECE, (q + 1) * PIECE)
+                    nc.vector.tensor_tensor(
+                        a2[1][:, 1, part], a1[:].indirect(p3[:, q * cols : (q + 1) * cols]), receipt[:, part], ALU.add
+                    )
+                    round_pair(1, q)
+                    if q > 0:
+                        flags(q - 1)
+                flags(PIECES - 1)

@@ -26,6 +26,7 @@ OUT_BLOCKS = N // P
 PIECE = 128
 PIECES = KEPT // PIECE
 LIVE0 = 96
+W1_BYTES = PACK * H * 4
 
 
 def tile_list_duplicate_claim_flags_kernel(
@@ -36,19 +37,18 @@ def tile_list_duplicate_claim_flags_kernel(
     with ExitStack() as ctx:
         keep = ctx.enter_context(tc.tile_pool(name="keep", bufs=1))
         ring = ctx.enter_context(tc.tile_pool(name="ring", bufs=2))
-        psum = ctx.enter_context(tc.psum_pool(name="psum", bufs=8))
+        shared = ctx.enter_context(tc.tile_pool(name="shared", bufs=1))
+        psum = ctx.enter_context(tc.psum_pool(name="psum", bufs=1))
 
         def scale_rows(dst, src, queue):
-            nc.vector.memset(dst[:].rearrange("p a n -> p (a n)").bitcast(I32), 0)
+            nc.vector.memset(dst.rearrange("p a n -> p (a n)").bitcast(I32), 0)
             for q in range(4):
                 queue.dma_start(
                     out=dst[32 * q : 32 * q + 4, :, :].bitcast(I32),
                     in_=src[:, 4 * q : 4 * q + 4, :].rearrange("a r n -> r a n").bitcast(I32),
                 )
 
-        w2_scale_raw = keep.tile([P, PASSES, H], U8, align_bytes=64)
-        scale_rows(w2_scale_raw, w2_scales, nc.scalar)
-        scale_window = keep.tile([P, T], U8, tag="scale_window_then_w1", align_bytes=64)
+        scale_window = keep.tile([P, T], U8, tag="scale_window", align_bytes=64)
         nc.vector.memset(scale_window[0:LIVE0, :].bitcast(I32), 0)
         nc.sync.dma_start(
             out=scale_window[LIVE0:P, :].bitcast(I32),
@@ -56,19 +56,28 @@ def tile_list_duplicate_claim_flags_kernel(
         )
         idx = keep.tile([P, S // PER_COL], U16)
         nc.sync.dma_start(idx[:], offs)
+        w2_scale_raw = keep.tile([P, H], U8, align_bytes=64)
+        nc.vector.memset(w2_scale_raw[0:LIVE0, :].bitcast(I32), 0)
+        nc.sync.dma_start(
+            out=w2_scale_raw[LIVE0:P, :].bitcast(I32),
+            in_=w2_scales.rearrange("a q n -> (a q) n").bitcast(I32),
+        )
 
         def load_words(a):
             words = keep.tile([P, T], I32, name="words%d" % a, tag="words%d" % a, align_bytes=64)
             nc.sync.dma_start(out=words[:], in_=tab_words[a].rearrange("p t i -> p (t i)").bitcast(I32))
             return words
 
-        def load_w1(a, tag):
-            raw = keep.tile([P, PACK, H], F32, name="w1_raw%d" % a, tag=tag, align_bytes=64)
+        def load_w1(a):
+            raw = shared.tile([P, PACK, H], F32, name="w1_raw%d" % a, offset=a * W1_BYTES, align_bytes=64)
             nc.sync.dma_start(
                 out=raw[:], in_=w1[a * P * PACK : (a + 1) * P * PACK, :].rearrange("(p j) c -> p j c", j=PACK)
             )
             return raw
 
+        w2_raw = keep.tile([P, PASSES, 2 * H], U8, tag="w2_raw", align_bytes=64)
+        nc.sync.dma_start(out=w2_raw[:].bitcast(I32), in_=w2_words.rearrange("a p n -> p a n").bitcast(I32))
+        word_windows = [load_words(0)]
         p2 = keep.tile([P, PAIRS // PER_COL], U16)
         nc.sync.dma_start(p2[:], pos2)
         p4 = keep.tile([P, KEPT // PER_COL], U16)
@@ -77,36 +86,38 @@ def tile_list_duplicate_claim_flags_kernel(
         nc.sync.dma_start(p1[:], pos1)
         p3 = keep.tile([P, KEPT // PER_COL], U16)
         nc.sync.dma_start(p3[:], pos3)
-        word_windows = [load_words(0)]
-        w2_raw = keep.tile([P, PASSES, 2 * H], U8, align_bytes=64)
-        nc.sync.dma_start(out=w2_raw[:].bitcast(I32), in_=w2_words.rearrange("a p n -> p a n").bitcast(I32))
-        w1_raw = [load_w1(0, "w1_then_w4")]
         word_windows.append(load_words(1))
 
-        v_scales = keep.tile([P, PASSES, S], U8, align_bytes=64)
-        nc.gpsimd.memset(v_scales[:].rearrange("p a n -> p (a n)").bitcast(I32), 0)
+        v_scales = [keep.tile([P, S + H], U8, name="v_scales%d" % a, align_bytes=64) for a in range(PASSES)]
+        for a in range(PASSES):
+            nc.gpsimd.memset(v_scales[a][:].bitcast(I32), 0)
         sharp_sb = keep.tile([P, PACK], F32)
         nc.gpsimd.dma_start(out=sharp_sb[:], in_=sharp.rearrange("(p t) -> p t", t=PACK))
-        w4_scale = keep.tile([P, 1, N], U8, align_bytes=64)
-        scale_rows(w4_scale, w4_scales, nc.gpsimd)
-        wf_sb = keep.tile([P, OUT_BLOCKS], F32)
-        with nc.allow_non_contiguous_dma(reason="one weight for each output row"):
-            nc.gpsimd.dma_start(out=wf_sb[:], in_=wf.rearrange("(b p) -> p b", p=P))
 
-        picked_scales = keep.tile([P, S], U8, align_bytes=64)
+        picked_scales = shared.tile([P, S], U8, offset=W1_BYTES - S // 2, align_bytes=64)
         nc.vector.tensor_copy(picked_scales[:], scale_window[:].indirect(idx[:]))
+        rows = keep.tile([P, S + H], U8, align_bytes=64)
+        nc.vector.tensor_copy(
+            out=rows[:, S:].rearrange("p (t m) -> p t m", t=PACK),
+            in_=w2_scale_raw[:].rearrange("p (m t) -> p t m", t=PACK),
+        )
+        nc.vector.tensor_copy(out=rows[LIVE0:P, 0:S].bitcast(I32), in_=picked_scales[LIVE0:P, :].bitcast(I32))
 
         def place_scales(a):
             for q in range(4):
                 row = LIVE0 + 16 * a + 4 * q
                 nc.sync.dma_start(
-                    out=v_scales[32 * q : 32 * q + 4, a, :].bitcast(I32),
-                    in_=picked_scales[row : row + 4, :].bitcast(I32),
+                    out=v_scales[a][32 * q : 32 * q + 4, :].bitcast(I32),
+                    in_=rows[row : row + 4, :].bitcast(I32),
                 )
 
         place_scales(0)
-        w1_raw.append(load_w1(1, "scale_window_then_w1"))
+        w1_raw = [load_w1(a) for a in range(PASSES)]
         place_scales(1)
+        w2_codes = keep.tile([P, PASSES, PACK, 2 * P], U8, align_bytes=64)
+        nc.vector.tensor_copy(
+            out=w2_codes[:].bitcast(U16), in_=w2_raw[:].bitcast(U16).rearrange("p a (m t) -> p a t m", t=PACK)
+        )
 
         v_words = {}
 
@@ -116,7 +127,7 @@ def tile_list_duplicate_claim_flags_kernel(
             nc.vector.tensor_copy(
                 picked[:], word_windows[a][:].bitcast(U32).indirect(idx[:, s * cols : (s + 1) * cols])
             )
-            v_words[a, s] = picked
+            v_words[a, s] = picked[:]
 
         w1_codes, w1_scale = {}, {}
 
@@ -130,55 +141,75 @@ def tile_list_duplicate_claim_flags_kernel(
             )
             w1_codes[a, t], w1_scale[a, t] = codes, scale
 
+        picked0 = keep.tile([P, S], U32, align_bytes=64)
+        nc.vector.tensor_copy(picked0[:], word_windows[0][:].bitcast(U32).indirect(idx[:]))
         for s in range(SLICES):
-            gather_words(0, s)
+            v_words[0, s] = picked0[:, s * BANK : (s + 1) * BANK]
 
-        w2_codes = keep.tile([P, PASSES, PACK, 2 * P], U8, align_bytes=64)
-        w2_scale = keep.tile([P, PASSES, PACK, P], U8, align_bytes=64)
-        nc.vector.tensor_copy(
-            out=w2_codes[:].bitcast(U16), in_=w2_raw[:].bitcast(U16).rearrange("p a (m t) -> p a t m", t=PACK)
-        )
-        nc.vector.tensor_copy(out=w2_scale[:], in_=w2_scale_raw[:].rearrange("p a (m t) -> p a t m", t=PACK))
-        for t in range(PACK):
-            quantise_w1(0, t)
         for s in range(SLICES):
             gather_words(1, s)
-        for t in range(PACK):
-            quantise_w1(1, t)
 
         w3_raw = keep.tile([P, PACK, N], F32, tag="words0", align_bytes=64)
         nc.sync.dma_start(out=w3_raw[:], in_=w3.rearrange("(p j) n -> p j n", j=PACK))
-        w4_codes = keep.tile([P, 2 * N], U8, tag="w1_then_w4", align_bytes=64)
-        nc.sync.dma_start(out=w4_codes[:].bitcast(I32), in_=w4_words[0].bitcast(I32))
+        wf_sb = keep.tile([P, OUT_BLOCKS], F32, tag="words1", align_bytes=64)
+        with nc.allow_non_contiguous_dma(reason="one weight for each output row"):
+            nc.sync.dma_start(out=wf_sb[:], in_=wf.rearrange("(b p) -> p b", p=P))
 
-        h = [keep.tile([P, S], F32, name="h%d" % t) for t in range(PACK)]
-
-        def first_pass(t, s, a, by_w1, by_w2):
-            cols = slice(s * BANK, (s + 1) * BANK)
-            nc.tensor.matmul_mx(
-                out=by_w2[:], lhsT=w2_codes[:, a, t, :].bitcast(FP4X4), lhsT_scale=w2_scale[:, a, t, :],
-                rhs=v_words[a, s][:].bitcast(FP8X4), rhs_scale=v_scales[:, a, cols],
-                start=(a == 0), stop=(a == PASSES - 1),
-            )
-            nc.tensor.matmul_mx(
-                out=by_w1[:], lhsT=w1_codes[a, t][:].bitcast(FP8X4), lhsT_scale=w1_scale[a, t][:],
-                rhs=v_words[a, s][:].bitcast(FP8X4), rhs_scale=v_scales[:, a, cols],
-                start=(a == 0), stop=(a == PASSES - 1),
-            )
-
-        def h_slice(t, s):
-            by_w1 = psum.tile([P, BANK], F32, name="bank")
-            by_w2 = psum.tile([P, BANK], F32, name="bank")
-            for a in range(PASSES):
-                first_pass(t, s, a, by_w1, by_w2)
-            by_w2_sb = ring.tile([P, BANK], F32, name="by_w2_sb", bufs=4)
-            nc.scalar.copy(out=by_w2_sb[:], in_=by_w2[:])
-            nc.vector.tensor_tensor(h[t][:, s * BANK : (s + 1) * BANK], by_w1[:], by_w2_sb[:], ALU.max)
-
-        for s in range(SLICES):
-            h_slice(0, s)
-
+        h = {}
         a2 = [keep.tile([P, 2, KEPT], F32, name="a2_%d" % u) for u in range(2)]
+
+        def pass_w2(t, s, a, bank):
+            nc.tensor.matmul_mx(
+                out=bank[:], lhsT=w2_codes[:, a, t, :].bitcast(FP4X4), lhsT_scale=v_scales[a][:, S + t * P : S + (t + 1) * P],
+                rhs=v_words[a, s].bitcast(FP8X4), rhs_scale=v_scales[a][:, s * BANK : (s + 1) * BANK],
+                start=(a == 0), stop=(a == PASSES - 1),
+            )
+
+        def pass_w1(t, s, a, bank):
+            nc.tensor.matmul_mx(
+                out=bank[:], lhsT=w1_codes[a, t][:].bitcast(FP8X4), lhsT_scale=w1_scale[a, t][:],
+                rhs=v_words[a, s].bitcast(FP8X4), rhs_scale=v_scales[a][:, s * BANK : (s + 1) * BANK],
+                start=(a == 0), stop=(a == PASSES - 1),
+            )
+
+        def take_max(t, s, by_w1, by_w2):
+            if t > 0 and s == SLICES - 1:
+                by_w2_sb = a2[(t - 1) // 2][:, (t - 1) % 2, :]
+            else:
+                by_w2_sb = ring.tile([P, BANK], F32, name="by_w2_sb", bufs=4)[:]
+            nc.scalar.copy(out=by_w2_sb, in_=by_w2[:])
+            nc.vector.tensor_tensor(h[t][:, s * BANK : (s + 1) * BANK], by_w1[:], by_w2_sb, ALU.max)
+
+        def h_tile(t):
+            h[t] = keep.tile([P, S], F32, name="h")
+            by_w1 = [psum.tile([P, BANK], F32, name="bank%d" % s) for s in range(SLICES)]
+            by_w2 = [psum.tile([P, BANK], F32, name="bank%d" % (SLICES + s)) for s in range(SLICES)]
+            if t == 0:
+                for a in range(PASSES):
+                    quantise_w1(a, t)
+            if t == 0:
+                for s in range(SLICES):
+                    pass_w2(t, s, 0, by_w2[s])
+                for s in range(SLICES):
+                    pass_w1(t, s, 0, by_w1[s])
+                for s in range(SLICES):
+                    pass_w2(t, s, 1, by_w2[s])
+                    pass_w1(t, s, 1, by_w1[s])
+            else:
+                for s in range(SLICES):
+                    for a in range(PASSES):
+                        pass_w2(t, s, a, by_w2[s])
+                for s in range(SLICES):
+                    for a in range(PASSES):
+                        pass_w1(t, s, a, by_w1[s])
+            for s in range(SLICES):
+                take_max(t, s, by_w1[s], by_w2[s])
+            if t + 1 < PACK:
+                for a in range(PASSES):
+                    quantise_w1(a, t + 1)
+
+        h_tile(0)
+
         a2_grouped = [keep.tile([P, PIECE, PACK], BF16, name="a2_grouped%d" % q, align_bytes=64) for q in range(PIECES)]
 
         def round_pair(u, q):
@@ -200,18 +231,18 @@ def tile_list_duplicate_claim_flags_kernel(
                 out=w3_codes[:].bitcast(FP8X4), scales=w3_scale[:], in_=grouped[:].rearrange("p n j -> p (n j)")
             )
 
-        def flags(q):
+        def flags(q, w4_codes, w4_scale):
             codes = ring.tile([P, PIECE], U32, name="a2_codes", align_bytes=64)
             scale = ring.tile([P, PIECE], U8, name="a2_scale", align_bytes=64)
             nc.vector.quantize_mx(
                 out=codes[:].bitcast(FP8X4), scales=scale[:], in_=a2_grouped[q][:].rearrange("p j t -> p (j t)")
             )
-            by_w3 = psum.tile([P, OUT_BLOCKS, PIECE], F32, name="bank")
-            by_w4 = psum.tile([P, OUT_BLOCKS, PIECE], F32, name="bank")
+            by_w3 = psum.tile([P, OUT_BLOCKS, PIECE], F32, name="bank%d" % q)
+            by_w4 = psum.tile([P, OUT_BLOCKS, PIECE], F32, name="bank%d" % (SLICES + q))
             for b in range(OUT_BLOCKS):
                 nc.tensor.matmul_mx(
                     out=by_w4[:, b, :], lhsT=w4_codes[:, 2 * P * b : 2 * P * (b + 1)].bitcast(FP4X4),
-                    lhsT_scale=w4_scale[:, 0, P * b : P * (b + 1)],
+                    lhsT_scale=w4_scale[:, P * b : P * (b + 1)],
                     rhs=codes[:].bitcast(FP8X4), rhs_scale=scale[:], start=True, stop=True,
                 )
             for b in range(OUT_BLOCKS):
@@ -239,15 +270,21 @@ def tile_list_duplicate_claim_flags_kernel(
             nc.scalar.activation(out=bend[:], in_=second[:], func=ACT.Tanh, scale=sharp_sb[:, t : t + 1])
             receipt = ring.tile([P, KEPT], F32, name="receipt")
             nc.vector.tensor_copy(receipt[:], h[t][:].indirect(p4[:]))
-            if not last:
-                for s in range(SLICES // 2):
-                    h_slice(t + 1, s)
             a1 = ring.tile([P, PAIRS], F32, name="a1")
-            nc.vector.tensor_tensor(a1[:], h[t][:].indirect(p1[:]), bend[:], ALU.mult)
-            if not last:
-                for s in range(SLICES // 2, SLICES):
-                    h_slice(t + 1, s)
+            if last:
+                nc.vector.tensor_tensor(a1[:], h[t][:].indirect(p1[:]), bend[:], ALU.mult)
+            else:
+                first = ring.tile([P, PAIRS], F32, name="first")
+                nc.vector.tensor_copy(first[:], h[t][:].indirect(p1[:]))
+                nc.gpsimd.tensor_tensor(a1[:], first[:], bend[:], ALU.mult)
+                h_tile(t + 1)
                 nc.vector.tensor_tensor(a2[t // 2][:, t % 2, :], a1[:].indirect(p3[:]), receipt[:], ALU.add)
+            if t == PACK - 2:
+                w4_bytes = shared.tile([P, 3 * N], U8, offset=0, align_bytes=64)
+                w4_codes = w4_bytes[:, 0 : 2 * N]
+                w4_scale = w4_bytes[:, 2 * N : 3 * N]
+                nc.sync.dma_start(out=w4_codes.bitcast(I32), in_=w4_words[0].bitcast(I32))
+                scale_rows(w4_scale.rearrange("p (a n) -> p a n", a=1), w4_scales, nc.sync)
             if t == 1:
                 for q in range(PIECES):
                     round_pair(0, q)
@@ -261,5 +298,5 @@ def tile_list_duplicate_claim_flags_kernel(
                     )
                     round_pair(1, q)
                     if q > 0:
-                        flags(q - 1)
-                flags(PIECES - 1)
+                        flags(q - 1, w4_codes, w4_scale)
+                flags(PIECES - 1, w4_codes, w4_scale)

@@ -181,7 +181,7 @@ def tile_list_duplicate_claim_flags_kernel(
             nc.vector.tensor_tensor(h[t][:, s * BANK : (s + 1) * BANK], by_w1[:], by_w2_sb, ALU.max)
 
         def h_tile(t):
-            h[t] = keep.tile([P, S], F32, name="h")
+            h[t] = ring.tile([P, S], F32, name="h")
             by_w1 = [psum.tile([P, BANK], F32, name="bank%d" % s) for s in range(SLICES)]
             by_w2 = [psum.tile([P, BANK], F32, name="bank%d" % (SLICES + s)) for s in range(SLICES)]
             if t == 0:
@@ -232,8 +232,8 @@ def tile_list_duplicate_claim_flags_kernel(
             )
 
         def flags(q, w4_codes, w4_scale):
-            codes = ring.tile([P, PIECE], U32, name="a2_codes", align_bytes=64)
-            scale = ring.tile([P, PIECE], U8, name="a2_scale", align_bytes=64)
+            codes = ring.tile([P, PIECE], U32, name="a2_codes", bufs=PIECES, align_bytes=64)
+            scale = ring.tile([P, PIECE], U8, name="a2_scale", bufs=PIECES, align_bytes=64)
             nc.vector.quantize_mx(
                 out=codes[:].bitcast(FP8X4), scales=scale[:], in_=a2_grouped[q][:].rearrange("p j t -> p (j t)")
             )
@@ -251,11 +251,14 @@ def tile_list_duplicate_claim_flags_kernel(
                     lhsT_scale=w3_scale[:, P * b : P * (b + 1)],
                     rhs=codes[:].bitcast(FP8X4), rhs_scale=scale[:], start=True, stop=True,
                 )
-            by_w4_sb = ring.tile([P, OUT_BLOCKS, PIECE], F32, name="by_w4_sb")
+            by_w4_sb = ring.tile([P, OUT_BLOCKS, PIECE], F32, name="by_w4_sb", bufs=PIECES)
             nc.scalar.copy(out=by_w4_sb[:], in_=by_w4[:])
-            top = ring.tile([P, OUT_BLOCKS, PIECE], F32, name="top")
+            top = ring.tile([P, OUT_BLOCKS, PIECE], F32, name="top", bufs=PIECES)
             nc.vector.tensor_tensor(top[:], by_w3[:], by_w4_sb[:], ALU.max)
-            weighted = ring.tile([P, OUT_BLOCKS, PIECE], F32, name="weighted", bufs=4)
+            return top
+
+        def store(q, top):
+            weighted = ring.tile([P, OUT_BLOCKS, PIECE], F32, name="weighted", bufs=PIECES)
             for b in range(OUT_BLOCKS):
                 nc.scalar.activation(out=weighted[:, b, :], in_=top[:, b, :], func=ACT.Copy, scale=wf_sb[:, b : b + 1])
             nc.sync.dma_start(
@@ -271,12 +274,8 @@ def tile_list_duplicate_claim_flags_kernel(
             receipt = ring.tile([P, KEPT], F32, name="receipt")
             nc.vector.tensor_copy(receipt[:], h[t][:].indirect(p4[:]))
             a1 = ring.tile([P, PAIRS], F32, name="a1")
-            if last:
-                nc.vector.tensor_tensor(a1[:], h[t][:].indirect(p1[:]), bend[:], ALU.mult)
-            else:
-                first = ring.tile([P, PAIRS], F32, name="first")
-                nc.vector.tensor_copy(first[:], h[t][:].indirect(p1[:]))
-                nc.gpsimd.tensor_tensor(a1[:], first[:], bend[:], ALU.mult)
+            nc.vector.tensor_tensor(a1[:], h[t][:].indirect(p1[:]), bend[:], ALU.mult)
+            if not last:
                 h_tile(t + 1)
                 nc.vector.tensor_tensor(a2[t // 2][:, t % 2, :], a1[:].indirect(p3[:]), receipt[:], ALU.add)
             if t == PACK - 2:
@@ -297,6 +296,6 @@ def tile_list_duplicate_claim_flags_kernel(
                         a2[1][:, 1, part], a1[:].indirect(p3[:, q * cols : (q + 1) * cols]), receipt[:, part], ALU.add
                     )
                     round_pair(1, q)
-                    if q > 0:
-                        flags(q - 1, w4_codes, w4_scale)
-                flags(PIECES - 1, w4_codes, w4_scale)
+                tops = [flags(q, w4_codes, w4_scale) for q in range(PIECES)]
+                for q in range(PIECES):
+                    store(q, tops[q])

@@ -26,7 +26,6 @@ OUT_BLOCKS = N // P
 PIECE = 128
 PIECES = KEPT // PIECE
 LIVE0 = 96
-W1_BYTES = PACK * H * 4
 
 
 def tile_list_duplicate_claim_flags_kernel(
@@ -37,7 +36,6 @@ def tile_list_duplicate_claim_flags_kernel(
     with ExitStack() as ctx:
         keep = ctx.enter_context(tc.tile_pool(name="keep", bufs=1))
         ring = ctx.enter_context(tc.tile_pool(name="ring", bufs=2))
-        shared = ctx.enter_context(tc.tile_pool(name="shared", bufs=1))
         psum = ctx.enter_context(tc.psum_pool(name="psum", bufs=1))
 
         def scale_rows(dst, src, queue):
@@ -69,7 +67,7 @@ def tile_list_duplicate_claim_flags_kernel(
             return words
 
         def load_w1(a):
-            raw = shared.tile([P, PACK, H], F32, name="w1_raw%d" % a, offset=a * W1_BYTES, align_bytes=64)
+            raw = keep.tile([P, PACK, H], F32, name="w1_raw%d" % a, tag="w1_raw%d" % a, align_bytes=64)
             nc.sync.dma_start(
                 out=raw[:], in_=w1[a * P * PACK : (a + 1) * P * PACK, :].rearrange("(p j) c -> p j c", j=PACK)
             )
@@ -86,7 +84,7 @@ def tile_list_duplicate_claim_flags_kernel(
         nc.sync.dma_start(p1[:], pos1)
         p3 = keep.tile([P, KEPT // PER_COL], U16)
         nc.sync.dma_start(p3[:], pos3)
-        word_windows.append(load_words(1))
+        w1_raw = [load_w1(a) for a in range(PASSES)]
 
         v_scales = [keep.tile([P, S + H], U8, name="v_scales%d" % a, align_bytes=64) for a in range(PASSES)]
         for a in range(PASSES):
@@ -94,7 +92,7 @@ def tile_list_duplicate_claim_flags_kernel(
         sharp_sb = keep.tile([P, PACK], F32)
         nc.gpsimd.dma_start(out=sharp_sb[:], in_=sharp.rearrange("(p t) -> p t", t=PACK))
 
-        picked_scales = shared.tile([P, S], U8, offset=W1_BYTES - S // 2, align_bytes=64)
+        picked_scales = keep.tile([P, S], U8, tag="words1", align_bytes=64)
         nc.vector.tensor_copy(picked_scales[:], scale_window[:].indirect(idx[:]))
         rows = keep.tile([P, S + H], U8, align_bytes=64)
         nc.vector.tensor_copy(
@@ -112,7 +110,7 @@ def tile_list_duplicate_claim_flags_kernel(
                 )
 
         place_scales(0)
-        w1_raw = [load_w1(a) for a in range(PASSES)]
+        word_windows.append(load_words(1))
         place_scales(1)
         w2_codes = keep.tile([P, PASSES, PACK, 2 * P], U8, align_bytes=64)
         nc.vector.tensor_copy(
@@ -132,7 +130,7 @@ def tile_list_duplicate_claim_flags_kernel(
         w1_codes, w1_scale = {}, {}
 
         def quantise_w1(a, t):
-            grouped = ring.tile([P, P, PACK], BF16, name="w1_grouped", bufs=4, align_bytes=64)
+            grouped = ring.tile([P, P, PACK], BF16, name="w1_grouped", bufs=PASSES * PACK, align_bytes=64)
             nc.scalar.copy(out=grouped[:], in_=w1_raw[a][:].rearrange("p j (m t) -> p t m j", t=PACK)[:, t, :, :])
             codes = keep.tile([P, P], U32, name="w1_codes%d_%d" % (a, t), align_bytes=64)
             scale = keep.tile([P, P], U8, name="w1_scale%d_%d" % (a, t), align_bytes=64)
@@ -146,12 +144,15 @@ def tile_list_duplicate_claim_flags_kernel(
         for s in range(SLICES):
             v_words[0, s] = picked0[:, s * BANK : (s + 1) * BANK]
 
+        for t in range(PACK):
+            for a in range(PASSES):
+                quantise_w1(a, t)
         for s in range(SLICES):
             gather_words(1, s)
 
         w3_raw = keep.tile([P, PACK, N], F32, tag="words0", align_bytes=64)
         nc.sync.dma_start(out=w3_raw[:], in_=w3.rearrange("(p j) n -> p j n", j=PACK))
-        wf_sb = keep.tile([P, OUT_BLOCKS], F32, tag="words1", align_bytes=64)
+        wf_sb = keep.tile([P, OUT_BLOCKS], F32, tag="w1_raw1", align_bytes=64)
         with nc.allow_non_contiguous_dma(reason="one weight for each output row"):
             nc.sync.dma_start(out=wf_sb[:], in_=wf.rearrange("(b p) -> p b", p=P))
 
@@ -185,9 +186,6 @@ def tile_list_duplicate_claim_flags_kernel(
             by_w1 = [psum.tile([P, BANK], F32, name="bank%d" % s) for s in range(SLICES)]
             by_w2 = [psum.tile([P, BANK], F32, name="bank%d" % (SLICES + s)) for s in range(SLICES)]
             if t == 0:
-                for a in range(PASSES):
-                    quantise_w1(a, t)
-            if t == 0:
                 for s in range(SLICES):
                     pass_w2(t, s, 0, by_w2[s])
                 for s in range(SLICES):
@@ -204,9 +202,6 @@ def tile_list_duplicate_claim_flags_kernel(
                         pass_w1(t, s, a, by_w1[s])
             for s in range(SLICES):
                 take_max(t, s, by_w1[s], by_w2[s])
-            if t + 1 < PACK:
-                for a in range(PASSES):
-                    quantise_w1(a, t + 1)
 
         h_tile(0)
 
@@ -279,7 +274,7 @@ def tile_list_duplicate_claim_flags_kernel(
                 h_tile(t + 1)
                 nc.vector.tensor_tensor(a2[t // 2][:, t % 2, :], a1[:].indirect(p3[:]), receipt[:], ALU.add)
             if t == PACK - 2:
-                w4_bytes = shared.tile([P, 3 * N], U8, offset=0, align_bytes=64)
+                w4_bytes = keep.tile([P, 3 * N], U8, tag="w1_raw0", align_bytes=64)
                 w4_codes = w4_bytes[:, 0 : 2 * N]
                 w4_scale = w4_bytes[:, 2 * N : 3 * N]
                 nc.sync.dma_start(out=w4_codes.bitcast(I32), in_=w4_words[0].bitcast(I32))

from contextlib import ExitStack

import concourse.mybir as mybir

K, H, N, T, S, PAIRS, KEPT = 1024, 512, 384, 4096, 2048, 1024, 512
FLOPS = 2 * 2 * K * H * S + 2 * 2 * H * N * KEPT

F32 = mybir.dt.float32
BF16 = mybir.dt.bfloat16
I32 = mybir.dt.int32
U32 = mybir.dt.uint32
U16 = mybir.dt.uint16
U8 = mybir.dt.uint8
FP8X4 = mybir.dt.float8_e4m3fn_x4
FP4X4 = mybir.dt.float4_e2m1fn_x4
ALU = mybir.AluOpType
ACT = mybir.ActivationFunctionType

P = 128
PACK = 4
PASSES = K // (P * PACK)
BANK = 512
SLICES = S // BANK
PER_COL = 16
OUT_BLOCKS = N // P
PIECE = 128
PIECES = KEPT // PIECE
LIVE0 = 96


def tile_list_duplicate_claim_flags_kernel(
    tc, tab_words, tab_scales, offs, w1, w2_words, w2_scales, sharp,
    pos1, pos2, pos3, pos4, w3, w4_words, w4_scales, wf, out,
):
    nc = tc.nc
    with ExitStack() as ctx:
        keep = ctx.enter_context(tc.tile_pool(name="keep", bufs=1))
        ring = ctx.enter_context(tc.tile_pool(name="ring", bufs=2))
        psum = ctx.enter_context(tc.psum_pool(name="psum", bufs=1))

        def scale_rows(dst, src, queue):
            nc.vector.memset(dst.rearrange("p a n -> p (a n)").bitcast(I32), 0)
            for q in range(4):
                queue.dma_start(
                    out=dst[32 * q : 32 * q + 4, :, :].bitcast(I32),
                    in_=src[:, 4 * q : 4 * q + 4, :].rearrange("a r n -> r a n").bitcast(I32),
                )

        scale_window = keep.tile([P, T], U8, tag="scale_window", align_bytes=64)
        nc.vector.memset(scale_window[0:LIVE0, :].bitcast(I32), 0)
        nc.sync.dma_start(
            out=scale_window[LIVE0:P, :].bitcast(I32),
            in_=tab_scales.rearrange("a q t -> (a q) t").bitcast(I32),
        )
        idx = keep.tile([P, S // PER_COL], U16)
        nc.sync.dma_start(idx[:], offs)
        w2_scale_raw = keep.tile([P, H], U8, align_bytes=64)
        nc.vector.memset(w2_scale_raw[0:LIVE0, :].bitcast(I32), 0)
        nc.sync.dma_start(
            out=w2_scale_raw[LIVE0:P, :].bitcast(I32),
            in_=w2_scales.rearrange("a q n -> (a q) n").bitcast(I32),
        )

        def load_words(a):
            words = keep.tile([P, T], I32, name="words%d" % a, tag="words%d" % a, align_bytes=64)
            nc.sync.dma_start(out=words[:], in_=tab_words[a].rearrange("p t i -> p (t i)").bitcast(I32))
            return words

        def load_w1(a):
            raw = keep.tile([P, PACK, H], F32, name="w1_raw%d" % a, tag="w1_raw%d" % a, align_bytes=64)
            nc.sync.dma_start(
                out=raw[:], in_=w1[a * P * PACK : (a + 1) * P * PACK, :].rearrange("(p j) c -> p j c", j=PACK)
            )
            return raw

        w2_raw = keep.tile([P, PASSES, 2 * H], U8, tag="w2_raw", align_bytes=64)
        nc.sync.dma_start(out=w2_raw[:].bitcast(I32), in_=w2_words.rearrange("a p n -> p a n").bitcast(I32))
        word_windows = [load_words(0)]
        p2 = keep.tile([P, PAIRS // PER_COL], U16)
        nc.sync.dma_start(p2[:], pos2)
        p4 = keep.tile([P, KEPT // PER_COL], U16)
        nc.sync.dma_start(p4[:], pos4)
        p1 = keep.tile([P, PAIRS // PER_COL], U16)
        nc.sync.dma_start(p1[:], pos1)
        p3 = keep.tile([P, KEPT // PER_COL], U16)
        nc.sync.dma_start(p3[:], pos3)
        w1_raw = [load_w1(a) for a in range(PASSES)]

        v_scales = [keep.tile([P, S + H], U8, name="v_scales%d" % a, align_bytes=64) for a in range(PASSES)]
        for a in range(PASSES):
            nc.gpsimd.memset(v_scales[a][:].bitcast(I32), 0)
        sharp_sb = keep.tile([P, PACK], F32)
        nc.gpsimd.dma_start(out=sharp_sb[:], in_=sharp.rearrange("(p t) -> p t", t=PACK))

        picked_scales = keep.tile([P, S], U8, tag="words1", align_bytes=64)
        nc.vector.tensor_copy(picked_scales[:], scale_window[:].indirect(idx[:]))
        rows = keep.tile([P, S + H], U8, align_bytes=64)
        nc.vector.tensor_copy(
            out=rows[:, S:].rearrange("p (t m) -> p t m", t=PACK),
            in_=w2_scale_raw[:].rearrange("p (m t) -> p t m", t=PACK),
        )
        nc.vector.tensor_copy(out=rows[LIVE0:P, 0:S].bitcast(I32), in_=picked_scales[LIVE0:P, :].bitcast(I32))

        def place_scales(a):
            for q in range(4):
                row = LIVE0 + 16 * a + 4 * q
                nc.sync.dma_start(
                    out=v_scales[a][32 * q : 32 * q + 4, :].bitcast(I32),
                    in_=rows[row : row + 4, :].bitcast(I32),
                )

        place_scales(0)
        word_windows.append(load_words(1))
        place_scales(1)
        w2_codes = keep.tile([P, PASSES, PACK, 2 * P], U8, align_bytes=64)
        nc.vector.tensor_copy(
            out=w2_codes[:].bitcast(U16), in_=w2_raw[:].bitcast(U16).rearrange("p a (m t) -> p a t m", t=PACK)
        )

        v_words = {}

        def gather_words(a, s):
            picked = keep.tile([P, BANK], U32, name="v_words%d_%d" % (a, s), align_bytes=64)
            cols = BANK // PER_COL
            nc.vector.tensor_copy(
                picked[:], word_windows[a][:].bitcast(U32).indirect(idx[:, s * cols : (s + 1) * cols])
            )
            v_words[a, s] = picked[:]

        w1_codes, w1_scale = {}, {}

        def quantise_w1(a, t):
            grouped = ring.tile([P, P, PACK], BF16, name="w1_grouped", bufs=PASSES * PACK, align_bytes=64)
            nc.scalar.copy(out=grouped[:], in_=w1_raw[a][:].rearrange("p j (m t) -> p t m j", t=PACK)[:, t, :, :])
            codes = keep.tile([P, P], U32, name="w1_codes%d_%d" % (a, t), align_bytes=64)
            scale = keep.tile([P, P], U8, name="w1_scale%d_%d" % (a, t), align_bytes=64)
            nc.vector.quantize_mx(
                out=codes[:].bitcast(FP8X4), scales=scale[:], in_=grouped[:].rearrange("p m j -> p (m j)")
            )
            w1_codes[a, t], w1_scale[a, t] = codes, scale

        picked0 = keep.tile([P, S], U32, align_bytes=64)
        nc.vector.tensor_copy(picked0[:], word_windows[0][:].bitcast(U32).indirect(idx[:]))
        for s in range(SLICES):
            v_words[0, s] = picked0[:, s * BANK : (s + 1) * BANK]

        for t in range(PACK):
            for a in range(PASSES):
                quantise_w1(a, t)
        for s in range(SLICES):
            gather_words(1, s)

        w3_raw = keep.tile([P, PACK, N], F32, tag="words0", align_bytes=64)
        nc.sync.dma_start(out=w3_raw[:], in_=w3.rearrange("(p j) n -> p j n", j=PACK))
        wf_sb = keep.tile([P, OUT_BLOCKS], F32, tag="w1_raw1", align_bytes=64)
        with nc.allow_non_contiguous_dma(reason="one weight for each output row"):
            nc.sync.dma_start(out=wf_sb[:], in_=wf.rearrange("(b p) -> p b", p=P))

        h = {}
        a2 = [keep.tile([P, 2, KEPT], F32, name="a2_%d" % u) for u in range(2)]

        def pass_w2(t, s, a, bank):
            nc.tensor.matmul_mx(
                out=bank[:], lhsT=w2_codes[:, a, t, :].bitcast(FP4X4), lhsT_scale=v_scales[a][:, S + t * P : S + (t + 1) * P],
                rhs=v_words[a, s].bitcast(FP8X4), rhs_scale=v_scales[a][:, s * BANK : (s + 1) * BANK],
                start=(a == 0), stop=(a == PASSES - 1),
            )

        def pass_w1(t, s, a, bank):
            nc.tensor.matmul_mx(
                out=bank[:], lhsT=w1_codes[a, t][:].bitcast(FP8X4), lhsT_scale=w1_scale[a, t][:],
                rhs=v_words[a, s].bitcast(FP8X4), rhs_scale=v_scales[a][:, s * BANK : (s + 1) * BANK],
                start=(a == 0), stop=(a == PASSES - 1),
            )

        def take_max(t, s, by_w1, by_w2):
            if t > 0 and s == SLICES - 1:
                by_w2_sb = a2[(t - 1) // 2][:, (t - 1) % 2, :]
            else:
                by_w2_sb = ring.tile([P, BANK], F32, name="by_w2_sb", bufs=4)[:]
            nc.scalar.copy(out=by_w2_sb, in_=by_w2[:])
            nc.vector.tensor_tensor(h[t][:, s * BANK : (s + 1) * BANK], by_w1[:], by_w2_sb, ALU.max)

        def h_tile(t):
            h[t] = ring.tile([P, S], F32, name="h")
            by_w1 = [psum.tile([P, BANK], F32, name="bank%d" % s) for s in range(SLICES)]
            by_w2 = [psum.tile([P, BANK], F32, name="bank%d" % (SLICES + s)) for s in range(SLICES)]
            if t == 0:
                for s in range(SLICES):
                    pass_w2(t, s, 0, by_w2[s])
                for s in range(SLICES):
                    pass_w1(t, s, 0, by_w1[s])
                for s in range(SLICES):
                    pass_w2(t, s, 1, by_w2[s])
                    pass_w1(t, s, 1, by_w1[s])
            else:
                for s in range(SLICES):
                    for a in range(PASSES):
                        pass_w2(t, s, a, by_w2[s])
                for s in range(SLICES):
                    for a in range(PASSES):
                        pass_w1(t, s, a, by_w1[s])
            for s in range(SLICES):
                take_max(t, s, by_w1[s], by_w2[s])

        h_tile(0)

        a2_grouped = [keep.tile([P, PIECE, PACK], BF16, name="a2_grouped%d" % q, align_bytes=64) for q in range(PIECES)]

        def round_pair(u, q):
            nc.scalar.copy(
                out=a2_grouped[q][:, :, 2 * u : 2 * u + 2],
                in_=a2[u][:, :, q * PIECE : (q + 1) * PIECE].rearrange("p e j -> p j e"),
            )

        w3_codes = keep.tile([P, N], U32, align_bytes=64)
        w3_scale = keep.tile([P, N], U8, align_bytes=64)

        def quantise_w3():
            grouped = keep.tile([P, N, PACK], BF16, name="w3_grouped", align_bytes=64)
            nc.scalar.copy(
                out=grouped[:].rearrange("p (c i) j -> p c j i", i=4),
                in_=w3_raw[:].rearrange("p j (c i) -> p c j i", i=4),
            )
            nc.vector.quantize_mx(
                out=w3_codes[:].bitcast(FP8X4), scales=w3_scale[:], in_=grouped[:].rearrange("p n j -> p (n j)")
            )

        def flags(q, w4_codes, w4_scale):
            codes = ring.tile([P, PIECE], U32, name="a2_codes", bufs=PIECES, align_bytes=64)
            scale = ring.tile([P, PIECE], U8, name="a2_scale", bufs=PIECES, align_bytes=64)
            nc.vector.quantize_mx(
                out=codes[:].bitcast(FP8X4), scales=scale[:], in_=a2_grouped[q][:].rearrange("p j t -> p (j t)")
            )
            by_w3 = psum.tile([P, OUT_BLOCKS, PIECE], F32, name="bank%d" % q)
            by_w4 = psum.tile([P, OUT_BLOCKS, PIECE], F32, name="bank%d" % (SLICES + q))
            for b in range(OUT_BLOCKS):
                nc.tensor.matmul_mx(
                    out=by_w4[:, b, :], lhsT=w4_codes[:, 2 * P * b : 2 * P * (b + 1)].bitcast(FP4X4),
                    lhsT_scale=w4_scale[:, P * b : P * (b + 1)],
                    rhs=codes[:].bitcast(FP8X4), rhs_scale=scale[:], start=True, stop=True,
                )
            for b in range(OUT_BLOCKS):
                nc.tensor.matmul_mx(
                    out=by_w3[:, b, :], lhsT=w3_codes[:, P * b : P * (b + 1)].bitcast(FP8X4),
                    lhsT_scale=w3_scale[:, P * b : P * (b + 1)],
                    rhs=codes[:].bitcast(FP8X4), rhs_scale=scale[:], start=True, stop=True,
                )
            by_w4_sb = ring.tile([P, OUT_BLOCKS, PIECE], F32, name="by_w4_sb", bufs=PIECES)
            nc.scalar.copy(out=by_w4_sb[:], in_=by_w4[:])
            top = ring.tile([P, OUT_BLOCKS, PIECE], F32, name="top", bufs=PIECES)
            nc.vector.tensor_tensor(top[:], by_w3[:], by_w4_sb[:], ALU.max)
            return top

        def store(q, top):
            weighted = ring.tile([P, OUT_BLOCKS, PIECE], F32, name="weighted", bufs=PIECES)
            for b in range(OUT_BLOCKS):
                nc.scalar.activation(out=weighted[:, b, :], in_=top[:, b, :], func=ACT.Copy, scale=wf_sb[:, b : b + 1])
            nc.sync.dma_start(
                out=out.rearrange("(b p) j -> p b j", p=P)[:, :, q * PIECE : (q + 1) * PIECE], in_=weighted[:]
            )

        for t in range(PACK):
            last = t == PACK - 1
            second = ring.tile([P, PAIRS], F32, name="second")
            nc.vector.tensor_copy(second[:], h[t][:].indirect(p2[:]))
            bend = ring.tile([P, PAIRS], F32, name="bend")
            nc.scalar.activation(out=bend[:], in_=second[:], func=ACT.Tanh, scale=sharp_sb[:, t : t + 1])
            receipt = ring.tile([P, KEPT], F32, name="receipt")
            nc.vector.tensor_copy(receipt[:], h[t][:].indirect(p4[:]))
            a1 = ring.tile([P, PAIRS], F32, name="a1")
            nc.vector.tensor_tensor(a1[:], h[t][:].indirect(p1[:]), bend[:], ALU.mult)
            if not last:
                h_tile(t + 1)
                nc.vector.tensor_tensor(a2[t // 2][:, t % 2, :], a1[:].indirect(p3[:]), receipt[:], ALU.add)
            if t == PACK - 2:
                w4_bytes = keep.tile([P, 3 * N], U8, tag="w1_raw0", align_bytes=64)
                w4_codes = w4_bytes[:, 0 : 2 * N]
                w4_scale = w4_bytes[:, 2 * N : 3 * N]
                nc.sync.dma_start(out=w4_codes.bitcast(I32), in_=w4_words[0].bitcast(I32))
                scale_rows(w4_scale.rearrange("p (a n) -> p a n", a=1), w4_scales, nc.sync)
            if t == 1:
                for q in range(PIECES):
                    round_pair(0, q)
                quantise_w3()
            if last:
                cols = PIECE // PER_COL
                for q in range(PIECES):
                    part = slice(q * PIECE, (q + 1) * PIECE)
                    nc.vector.tensor_tensor(
                        a2[1][:, 1, part], a1[:].indirect(p3[:, q * cols : (q + 1) * cols]), receipt[:, part], ALU.add
                    )
                    round_pair(1, q)
                tops = [flags(q, w4_codes, w4_scale) for q in range(PIECES)]
                for q in range(PIECES):
                    store(q, tops[q])
